import numpy as np
import ml_dtypes


def mxq(x, axis, fmt="e4m3"):
    dtype, down = {"e4m3": (ml_dtypes.float8_e4m3fn, 7), "e5m2": (ml_dtypes.float8_e5m2, 14)}[fmt]
    v = np.moveaxis(np.asarray(x, np.float32).astype(ml_dtypes.bfloat16).astype(np.float64), axis, -1)
    blocks = v.reshape(v.shape[:-1] + (-1, 32))
    amax = np.abs(blocks).max(-1, keepdims=True)
    byte = np.maximum(np.where(amax > 0, np.frexp(amax)[1] - 1 + 127, 0) - down, 1)
    scale = np.exp2(byte - 127.0)
    codes = (blocks / scale).astype(np.float32).astype(dtype).astype(np.float64)
    return np.moveaxis((codes * scale).reshape(v.shape), -1, axis)


WIDE = False


def mx_kscale(k):
    if not WIDE:
        return np.ones(k)
    levels = np.array([10, -10, 5, -5, 0])
    if k % 512:
        return np.exp2(np.random.permutation(np.resize(levels, k // 32))).repeat(32)
    a = np.empty((k // 512, 16))
    for p in range(k // 512):
        a[p, :8] = np.random.permutation(np.resize(levels, 8))
        for g in range(8):
            far = levels[np.abs(levels - a[p, g]) >= 10]
            a[p, g + 8] = far[np.random.randint(len(far))]
    return np.exp2(a.ravel()).repeat(32)


def f64(x):
    return np.asarray(x).astype(np.float64)


def striped(idx):
    return np.tile(idx.reshape(-1, 16).T, (8, 1)).astype(np.uint16)


def unstriped(offs):
    return offs[:16].T.reshape(-1).astype(np.int64)


def striped8(idx):
    return np.concatenate([x.reshape(-1, 16).T for x in idx]).astype(np.uint16)


def runs(offs, k):
    lists = np.stack([offs[16 * r : 16 * r + 16].T.reshape(-1) for r in range(8)]).astype(np.int64)
    return lists[np.arange(k) % 512 // 64]


def pack_weight(w):
    k, n = w.shape
    w = f64(np.asarray(w, np.float32).astype(ml_dtypes.bfloat16)).reshape(k // 32, 32, n)
    amax = np.abs(w).max(1)
    byte = np.clip(np.where(amax > 0, np.frexp(amax)[1] - 1 + 127 - 7, 1), 1, 254)
    scaled = (w * np.exp2(127.0 - byte)[:, None, :]).reshape(k, n).astype(np.float32)
    words = np.ascontiguousarray(scaled.reshape(k // 512, 128, 4, n).transpose(0, 1, 3, 2)).astype(ml_dtypes.float8_e4m3fn).view(np.uint8)
    return words, np.ascontiguousarray(byte.astype(np.uint8).reshape(k // 512, 16, n))


def unpack_weight(words, scales):
    g, p, n, _ = words.shape
    vals = np.ascontiguousarray(words).view(ml_dtypes.float8_e4m3fn).astype(np.float64) * np.repeat(np.exp2(scales.astype(np.float64) - 127.0), 8, axis=1)[..., None]
    return vals.transpose(0, 1, 3, 2).reshape(g * 512, n)


K, T, S, N, H, C = 512, 2048, 512, 512, 512, 512


def setup_inputs():
    n = np.random.standard_normal
    s = mx_kscale(K)[:, None]
    u = mx_kscale(S)
    packed_xT = pack_weight(n((K, T)) * s)
    return {
        "x_words": packed_xT[0],
        "x_scales": packed_xT[1],
        "w1": (n((K, H)) / np.sqrt(K) / s).astype(np.float32),
        "gn": (np.random.uniform(0.5, 1.5, (H, 1)) * u[:, None]).astype(np.float32),
        "w2": (n((H, N)) / np.sqrt(H) / u[:, None]).astype(np.float32),
        "gs": (np.random.uniform(0.5, 1.5, (K, 1)) / s).astype(np.float32),
        "offs": striped(np.random.permutation(T)[:S]),
        "n1": striped8(np.stack([np.random.permutation(S) for _ in range(8)])),
        "n2": striped8(np.stack([np.random.permutation(S) for _ in range(8)])),
        "n3": striped8(np.stack([np.random.permutation(S) for _ in range(8)])),
        "n4": striped8(np.stack([np.random.permutation(S) for _ in range(8)])),
        "n5": striped8(np.stack([np.random.permutation(S) for _ in range(8)])),
        "cand": striped(np.random.permutation(T)[:C]),
        "n6": striped(np.random.permutation(S)),
        "n7": striped(np.random.permutation(S)),
    }


def reference(x_words, x_scales, w1, gn, w2, gs, offs, n1, n2, n3, n4, n5, cand, n6, n7):
    xq = unpack_weight(x_words, x_scales)[:, unstriped(offs)]
    y = mxq(f64(w1), 0, "e4m3").T @ xq
    z = f64(gn) * (0.75 * (y * (y[np.arange(H)[:, None], runs(n1, H)]) + (y[np.arange(H)[:, None], runs(n2, H)]) * (y[np.arange(H)[:, None], runs(n3, H)])))
    a = mxq(f64(w2), 0, "e4m3").T @ mxq(z, 0, "e4m3")
    x_cand = unpack_weight(x_words, x_scales)[:, unstriped(cand)]
    z2 = f64(gs) * (0.75 * ((y - (y[np.arange(H)[:, None], runs(n4, H)])) * (y - (y[np.arange(H)[:, None], runs(n5, H)]))))
    b = 0.0625 * ((x_cand.T @ mxq(z2, 0, "e4m3")))
    return a * (np.tanh(b[:, unstriped(n6)] - b[:, unstriped(n7)]))

@@ -1,0 +1,215 @@
+from contextlib import ExitStack
+
+import concourse.mybir as mybir
+
+K, T, S, N, H, C = 512, 2048, 512, 512, 512, 512
+FLOPS = 2 * (K * H * S + H * N * S + K * C * S)
+
+F32 = mybir.dt.float32
+BF16 = mybir.dt.bfloat16
+I32 = mybir.dt.int32
+U32 = mybir.dt.uint32
+U16 = mybir.dt.uint16
+U8 = mybir.dt.uint8
+FP8X4 = mybir.dt.float8_e4m3fn_x4
+MULT = mybir.AluOpType.mult
+ADD = mybir.AluOpType.add
+SUBTRACT = mybir.AluOpType.subtract
+COPY = mybir.ActivationFunctionType.Copy
+TANH = mybir.ActivationFunctionType.Tanh
+
+P = 128
+PACK = 4
+HALF = S // 2
+LIST_GROUP = 16
+N2_TILES_ON_VECTOR = 1
+N7_TILES_ON_SCALAR = 2
+
+
+def halves(offsets):
+    k = HALF // LIST_GROUP
+    return [(slice(h * HALF, (h + 1) * HALF), offsets[:, h * k : (h + 1) * k]) for h in range(2)]
+
+
+def gather_scalar(nc, dst, window, offsets):
+    for cols, part in halves(offsets):
+        nc.scalar.activation(dst[:, cols], window[:].indirect(part), COPY)
+
+
+def gather_vector(nc, dst, window, offsets):
+    for cols, part in halves(offsets):
+        nc.vector.tensor_copy(dst[:, cols], window[:].indirect(part))
+
+
+def gather_fused(nc, dst, window, offsets, other, op):
+    for cols, part in halves(offsets):
+        nc.vector.tensor_tensor(dst[:, cols], window[:].indirect(part), other[:, cols], op)
+
+
+def combine_and_quantize(nc, pool, name, left, right, op):
+    grouped = pool.tile([P, S, PACK], BF16, name=name + "_grouped", align_bytes=64)
+    codes = pool.tile([P, S], U32, name=name + "_codes", align_bytes=64)
+    scales = pool.tile([P, S], U8, name=name + "_scales", align_bytes=64)
+    nc.vector.tensor_tensor(
+        grouped[:].rearrange("p (c i) t -> p c t i", i=4),
+        left[:].rearrange("p t (c i) -> p c t i", i=4),
+        right[:].rearrange("p t (c i) -> p c t i", i=4),
+        op,
+    )
+    nc.vector.quantize_mx(codes[:].bitcast(FP8X4), scales[:], grouped[:].rearrange("p j t -> p (j t)"))
+    return codes, scales
+
+
+def product(nc, bank, left_codes, left_scales, t, right_codes, right_scales):
+    cols = slice(t * P, (t + 1) * P)
+    nc.tensor.matmul_mx(
+        out=bank[:],
+        lhsT=left_codes[:, cols].bitcast(FP8X4),
+        lhsT_scale=left_scales[:, cols],
+        rhs=right_codes[:].bitcast(FP8X4),
+        rhs_scale=right_scales[:],
+        start=True,
+        stop=True,
+    )
+
+
+def tile_picked_fkcdjointbdotquad_none_p_kernel(
+    tc, x_words, x_scales, w1, gn, w2, gs, offs, n1, n2, n3, n4, n5, cand, n6, n7, out
+):
+    nc = tc.nc
+    with ExitStack() as ctx:
+        keep = ctx.enter_context(tc.tile_pool(name="keep", bufs=1))
+        ring = ctx.enter_context(tc.tile_pool(name="ring", bufs=2))
+        psum = ctx.enter_context(tc.psum_pool(name="psum", bufs=1))
+
+        def load_list(name, source):
+            offsets = keep.tile([P, S // LIST_GROUP], U16, name=name)
+            nc.sync.dma_start(offsets[:], source)
+            return offsets
+
+        def load_gain(name, source):
+            raw = keep.tile([P, PACK], F32, name=name + "_raw")
+            gain = keep.tile([P, PACK], F32, name=name)
+            nc.sync.dma_start(raw[:], source.rearrange("(p t) o -> p (t o)", t=PACK))
+            nc.vector.tensor_scalar(gain[:], raw[:], 0.75, None, MULT)
+            return gain
+
+        table_scales = keep.tile([P, T], U8, name="table_scales")
+        nc.vector.memset(table_scales[:].bitcast(I32), 0)
+        offs_sb = load_list("offs_sb", offs)
+        table_words = keep.tile([P, T], I32, name="table_words")
+        nc.sync.dma_start(table_words[:], x_words[0].rearrange("p n t -> p (n t)").bitcast(I32))
+        for q in range(4):
+            nc.scalar.dma_start(
+                table_scales[32 * q : 32 * q + 4, :].bitcast(I32), x_scales[0, 4 * q : 4 * q + 4, :].bitcast(I32)
+            )
+        w1_rows = w1.rearrange("(p j) c -> p j c", j=PACK)
+        w1_raw = []
+        for u in range(2):
+            part = keep.tile([P, PACK, H // 2], F32, name=f"w1_raw{u}")
+            nc.sync.dma_start(part[:], w1_rows[:, :, u * (H // 2) : (u + 1) * (H // 2)])
+            w1_raw.append(part)
+        cand_sb = load_list("cand_sb", cand)
+        gs_sb = load_gain("gs_sb", gs)
+        gn_sb = load_gain("gn_sb", gn)
+        n4_sb = load_list("n4_sb", n4)
+        n5_sb = load_list("n5_sb", n5)
+        n1_sb = load_list("n1_sb", n1)
+        w2_raw = keep.tile([P, PACK, N], F32, name="w2_raw")
+        nc.sync.dma_start(w2_raw[:], w2.rearrange("(p j) c -> p j c", j=PACK))
+        n2_sb = load_list("n2_sb", n2)
+        n3_sb = load_list("n3_sb", n3)
+        n6_sb = load_list("n6_sb", n6)
+        n7_sb = load_list("n7_sb", n7)
+
+        def pick_columns(name, offsets):
+            words = keep.tile([P, S], U32, name=name + "_words", align_bytes=64)
+            scales = keep.tile([P, S], U8, name=name + "_scales", align_bytes=64)
+            nc.vector.tensor_copy(scales[:], table_scales[:].indirect(offsets[:]))
+            nc.vector.tensor_copy(words[:], table_words[:].bitcast(U32).indirect(offsets[:]))
+            return words, scales
+
+        token_words, token_scales = pick_columns("token", offs_sb)
+
+        w1_grouped = keep.tile([P, PACK, P, PACK], BF16, name="w1_grouped", align_bytes=64)
+        w1_codes = keep.tile([P, H], U32, name="w1_codes", align_bytes=64)
+        w1_scales = keep.tile([P, H], U8, name="w1_scales", align_bytes=64)
+        for u, copy in enumerate((nc.scalar.copy, nc.vector.tensor_copy)):
+            copy(
+                w1_grouped[:, :, u * (P // 2) : (u + 1) * (P // 2), :].rearrange("p t m j -> p m j t"),
+                w1_raw[u][:].rearrange("p j (m t) -> p m j t", t=PACK),
+            )
+        for t in range(PACK):
+            cols = slice(t * P, (t + 1) * P)
+            nc.vector.quantize_mx(
+                w1_codes[:, cols].bitcast(FP8X4), w1_scales[:, cols], w1_grouped[:, t].rearrange("p m j -> p (m j)")
+            )
+        cand_words, cand_scales = pick_columns("cand", cand_sb)
+
+        d4 = keep.tile([P, PACK, S], F32, name="d4")
+        d5 = keep.tile([P, PACK, S], F32, name="d5")
+        p1 = keep.tile([P, PACK, S], F32, name="p1")
+        p3 = keep.tile([P, PACK, S], F32, name="p3")
+        y, y_gn, at_n2 = [], [], []
+        for t in range(PACK):
+            bank = psum.tile([P, S], F32, name=f"y_bank{t}", tag=f"low{t}")
+            product(nc, bank, w1_codes, w1_scales, t, token_words, token_scales)
+            y_t = keep.tile([P, S], F32, name=f"y{t}")
+            y_gs_t = keep.tile([P, S], F32, name=f"y_gs{t}")
+            y_gn_t = keep.tile([P, S], F32, name=f"y_gn{t}")
+            at_n4 = ring.tile([P, S], F32, name="at_n4")
+            at_n5 = ring.tile([P, S], F32, name="at_n5")
+            nc.scalar.activation(y_t[:], bank[:], COPY)
+            nc.scalar.activation(y_gs_t[:], bank[:], COPY, scale=gs_sb[:, t : t + 1])
+            nc.vector.tensor_scalar(y_gn_t[:], y_t[:], gn_sb[:, t : t + 1], None, MULT)
+            gather_scalar(nc, at_n4, y_t, n4_sb)
+            gather_scalar(nc, at_n5, y_gs_t, n5_sb)
+            gather_fused(nc, p1[:, t], y_t, n1_sb, y_gn_t, MULT)
+            nc.vector.tensor_tensor(d4[:, t], at_n4[:], y_t[:], SUBTRACT)
+            nc.vector.tensor_tensor(d5[:, t], at_n5[:], y_gs_t[:], SUBTRACT)
+            y.append(y_t)
+            y_gn.append(y_gn_t)
+            at_n2.append(keep.tile([P, S], F32, name=f"at_n2_{t}"))
+
+        w2_grouped = keep.tile([P, N, PACK], BF16, name="w2_grouped", align_bytes=64)
+        w2_codes = keep.tile([P, N], U32, name="w2_codes", align_bytes=64)
+        w2_scales = keep.tile([P, N], U8, name="w2_scales", align_bytes=64)
+        nc.vector.tensor_copy(
+            w2_grouped[:].rearrange("p (c i) j -> p c j i", i=4), w2_raw[:].rearrange("p j (c i) -> p c j i", i=4)
+        )
+        for t in range(N2_TILES_ON_VECTOR):
+            gather_vector(nc, at_n2[t], y_gn[t], n2_sb)
+        nc.vector.quantize_mx(w2_codes[:].bitcast(FP8X4), w2_scales[:], w2_grouped[:].rearrange("p c j -> p (c j)"))
+
+        z2_codes, z2_scales = combine_and_quantize(nc, keep, "z2", d4, d5, MULT)
+        b_banks = []
+        for m in range(C // P):
+            bank = psum.tile([P, S], F32, name=f"b_bank{m}")
+            product(nc, bank, cand_words, cand_scales, m, z2_codes, z2_scales)
+            b_banks.append(bank)
+
+        for t in range(PACK):
+            if t >= N2_TILES_ON_VECTOR:
+                gather_scalar(nc, at_n2[t], y_gn[t], n2_sb)
+            gather_fused(nc, p3[:, t], y[t], n3_sb, at_n2[t], MULT)
+        z_codes, z_scales = combine_and_quantize(nc, keep, "z", p1, p3, ADD)
+
+        for m in range(N // P):
+            a_bank = psum.tile([P, S], F32, name=f"a_bank{m}", tag=f"low{m}")
+            product(nc, a_bank, w2_codes, w2_scales, m, z_codes, z_scales)
+            b_m = keep.tile([P, S], F32, name=f"b{m}")
+            at_n6 = keep.tile([P, S], F32, name=f"at_n6_{m}")
+            gap = keep.tile([P, S], F32, name=f"gap{m}")
+            gate = keep.tile([P, S], F32, name=f"gate{m}")
+            result = keep.tile([P, S], F32, name=f"result{m}")
+            nc.scalar.activation(b_m[:], b_banks[m][:], COPY)
+            gather_scalar(nc, at_n6, b_m, n6_sb)
+            if m < N7_TILES_ON_SCALAR:
+                at_n7 = keep.tile([P, S], F32, name=f"at_n7_{m}")
+                gather_scalar(nc, at_n7, b_m, n7_sb)
+                nc.vector.tensor_tensor(gap[:], at_n7[:], at_n6[:], SUBTRACT)
+            else:
+                gather_fused(nc, gap, b_m, n7_sb, at_n6, SUBTRACT)
+            nc.scalar.activation(gate[:], gap[:], TANH, scale=-0.0625)
+            nc.vector.tensor_tensor(result[:], a_bank[:], gate[:], MULT)
+            nc.sync.dma_start(out[m * P : (m + 1) * P, :], result[:])

@@ -1,6 +1,7 @@
 from contextlib import ExitStack
 
 import concourse.mybir as mybir
+from concourse.masks import make_identity
 
 K, T, S, N, H, C = 512, 2048, 512, 512, 512, 512
 FLOPS = 2 * (K * H * S + H * N * S + K * C * S)
@@ -20,54 +21,21 @@ TANH = mybir.ActivationFunctionType.Tanh
 
 P = 128
 PACK = 4
-HALF = S // 2
+BANK = 512
+WINDOW = 2 * S
 LIST_GROUP = 16
-N2_TILES_ON_VECTOR = 1
-N7_TILES_ON_SCALAR = 2
+N5_TILES_ON_VECTOR = 1
+N7_TILES_ON_SCALAR = 0
 
 
-def halves(offsets):
-    k = HALF // LIST_GROUP
-    return [(slice(h * HALF, (h + 1) * HALF), offsets[:, h * k : (h + 1) * k]) for h in range(2)]
-
-
-def gather_scalar(nc, dst, window, offsets):
-    for cols, part in halves(offsets):
-        nc.scalar.activation(dst[:, cols], window[:].indirect(part), COPY)
-
-
-def gather_vector(nc, dst, window, offsets):
-    for cols, part in halves(offsets):
-        nc.vector.tensor_copy(dst[:, cols], window[:].indirect(part))
-
-
-def gather_fused(nc, dst, window, offsets, other, op):
-    for cols, part in halves(offsets):
-        nc.vector.tensor_tensor(dst[:, cols], window[:].indirect(part), other[:, cols], op)
-
-
-def combine_and_quantize(nc, pool, name, left, right, op):
-    grouped = pool.tile([P, S, PACK], BF16, name=name + "_grouped", align_bytes=64)
-    codes = pool.tile([P, S], U32, name=name + "_codes", align_bytes=64)
-    scales = pool.tile([P, S], U8, name=name + "_scales", align_bytes=64)
-    nc.vector.tensor_tensor(
-        grouped[:].rearrange("p (c i) t -> p c t i", i=4),
-        left[:].rearrange("p t (c i) -> p c t i", i=4),
-        right[:].rearrange("p t (c i) -> p c t i", i=4),
-        op,
-    )
-    nc.vector.quantize_mx(codes[:].bitcast(FP8X4), scales[:], grouped[:].rearrange("p j t -> p (j t)"))
-    return codes, scales
-
-
-def product(nc, bank, left_codes, left_scales, t, right_codes, right_scales):
+def product(nc, bank, left, t, right):
     cols = slice(t * P, (t + 1) * P)
     nc.tensor.matmul_mx(
         out=bank[:],
-        lhsT=left_codes[:, cols].bitcast(FP8X4),
-        lhsT_scale=left_scales[:, cols],
-        rhs=right_codes[:].bitcast(FP8X4),
-        rhs_scale=right_scales[:],
+        lhsT=left[0][:, cols].bitcast(FP8X4),
+        lhsT_scale=left[1][:, cols],
+        rhs=right[0][:].bitcast(FP8X4),
+        rhs_scale=right[1][:],
         start=True,
         stop=True,
     )
@@ -79,8 +47,10 @@ def tile_picked_fkcdjointbdotquad_none_p_kernel(
     nc = tc.nc
     with ExitStack() as ctx:
         keep = ctx.enter_context(tc.tile_pool(name="keep", bufs=1))
-        ring = ctx.enter_context(tc.tile_pool(name="ring", bufs=2))
         psum = ctx.enter_context(tc.psum_pool(name="psum", bufs=1))
+
+        def bank(name, number):
+            return psum.tile([P, BANK], F32, name=name, tag=f"bank{number}")
 
         def load_list(name, source):
             offsets = keep.tile([P, S // LIST_GROUP], U16, name=name)
@@ -88,128 +58,226 @@ def tile_picked_fkcdjointbdotquad_none_p_kernel(
             return offsets
 
         def load_gain(name, source):
-            raw = keep.tile([P, PACK], F32, name=name + "_raw")
             gain = keep.tile([P, PACK], F32, name=name)
-            nc.sync.dma_start(raw[:], source.rearrange("(p t) o -> p (t o)", t=PACK))
-            nc.vector.tensor_scalar(gain[:], raw[:], 0.75, None, MULT)
+            nc.gpsimd.dma_start(gain[:], source.rearrange("(p t) o -> p (t o)", t=PACK))
             return gain
+
+        def turn(dst, src, start=True, stop=True):
+            nc.tensor.matmul(dst, src, identity[:], start=start, stop=stop, is_transpose=True)
+
+        def gain_row(name, gain, number, tag):
+            spread = bank(name + "_bank", number)
+            for t in range(PACK):
+                turn(spread[:, t * P : (t + 1) * P], gain[:, t : t + 1].to_broadcast([P, P]))
+            row = keep.tile([P, 2, P, 2], F32, name=name, tag=tag)
+            nc.scalar.activation(row[:], spread[:].rearrange("j (u e p) -> j u p e", u=2, e=2), COPY, scale=0.75)
+            return row
+
+        def turned_sum(banks, e, left, right):
+            for half in range(2):
+                for b in range(2):
+                    cols = slice((2 * half + b) * P, (2 * half + b + 1) * P)
+                    dst = banks[half][:, (2 * b + e) * P : (2 * b + e + 1) * P]
+                    turn(dst, left[:, cols], start=True, stop=False)
+                    turn(dst, right[:, cols], start=False, stop=True)
+
+        def pairs(turned):
+            return turned[:].rearrange("j (b e p) -> j b p e", b=2, e=2)
+
+        def spread_row(row, u):
+            return row[:, u].unsqueeze(1).to_broadcast([P, 2, P, 2])
+
+        def turn_back(back, u, rounded):
+            words = rounded[:].rearrange("j b p e -> j (b p e)").bitcast(F32)
+            for b in range(2):
+                turn(back[:, (2 * u + b) * P : (2 * u + b + 1) * P], words[:, b * P : (b + 1) * P])
+
+        def quantize_halves(name, backs):
+            codes = keep.tile([P, S], U32, name=name + "_codes", align_bytes=64)
+            scales = keep.tile([P, S], U8, name=name + "_scales", align_bytes=64)
+            for half in range(2):
+                cols = slice(half * (S // 2), (half + 1) * (S // 2))
+                grouped = keep.tile([P, S // 2, PACK], BF16, name=f"{name}_grouped{half}", align_bytes=64)
+                nc.scalar.copy(grouped[:].bitcast(F32), backs[half][:].rearrange("p (u j) -> p j u", u=2))
+                nc.vector.quantize_mx(
+                    codes[:, cols].bitcast(FP8X4), scales[:, cols], grouped[:].rearrange("p j t -> p (j t)")
+                )
+            return codes, scales
 
         table_scales = keep.tile([P, T], U8, name="table_scales")
         nc.vector.memset(table_scales[:].bitcast(I32), 0)
-        offs_sb = load_list("offs_sb", offs)
-        table_words = keep.tile([P, T], I32, name="table_words")
-        nc.sync.dma_start(table_words[:], x_words[0].rearrange("p n t -> p (n t)").bitcast(I32))
         for q in range(4):
             nc.scalar.dma_start(
                 table_scales[32 * q : 32 * q + 4, :].bitcast(I32), x_scales[0, 4 * q : 4 * q + 4, :].bitcast(I32)
             )
+        offs_sb = load_list("offs_sb", offs)
+        table_words = keep.tile([P, T], I32, name="table_words")
+        nc.sync.dma_start(table_words[:], x_words[0].rearrange("p n t -> p (n t)").bitcast(I32))
         w1_rows = w1.rearrange("(p j) c -> p j c", j=PACK)
         w1_raw = []
         for u in range(2):
             part = keep.tile([P, PACK, H // 2], F32, name=f"w1_raw{u}")
             nc.sync.dma_start(part[:], w1_rows[:, :, u * (H // 2) : (u + 1) * (H // 2)])
             w1_raw.append(part)
-        cand_sb = load_list("cand_sb", cand)
         gs_sb = load_gain("gs_sb", gs)
         gn_sb = load_gain("gn_sb", gn)
-        n4_sb = load_list("n4_sb", n4)
+        cand_sb = load_list("cand_sb", cand)
         n5_sb = load_list("n5_sb", n5)
-        n1_sb = load_list("n1_sb", n1)
+        n4_sb = load_list("n4_sb", n4)
         w2_raw = keep.tile([P, PACK, N], F32, name="w2_raw")
         nc.sync.dma_start(w2_raw[:], w2.rearrange("(p j) c -> p j c", j=PACK))
+        n1_sb = load_list("n1_sb", n1)
+        identity = keep.tile([P, P], F32, name="identity")
+        make_identity(nc, identity[:])
+
+        def pick(name, table, dtype, offsets, tag=None):
+            picked = keep.tile([P, S], dtype, name=name, tag=tag or name, align_bytes=64)
+            nc.vector.tensor_copy(picked[:], table.indirect(offsets[:]))
+            return picked
+
+        token_scales = pick("token_scales", table_scales[:], U8, offs_sb)
+        token_words = pick("token_words", table_words[:].bitcast(U32), U32, offs_sb)
+        cand_scales = pick("cand_scales", table_scales[:], U8, cand_sb)
+
+        w1_grouped = keep.tile([P, PACK, P, PACK], BF16, name="w1_grouped", align_bytes=64)
+        w1_codes = keep.tile([P, H], U32, name="w1_codes", align_bytes=64)
+        w1_scales = keep.tile([P, H], U8, name="w1_scales", align_bytes=64)
+        for copy, u, first, last in (
+            (nc.scalar.copy, 0, 0, 64),
+            (nc.scalar.copy, 1, 0, 32),
+            (nc.vector.tensor_copy, 1, 32, 64),
+        ):
+            copy(
+                w1_grouped[:, :, 64 * u + first : 64 * u + last, :].rearrange("p t m j -> p m j t"),
+                w1_raw[u][:, :, PACK * first : PACK * last].rearrange("p j (m t) -> p m j t", t=PACK),
+            )
+        for t in (0, 2):
+            cols = slice(t * P, (t + 2) * P)
+            nc.vector.quantize_mx(
+                w1_codes[:, cols].bitcast(FP8X4),
+                w1_scales[:, cols],
+                w1_grouped[:, t : t + 2].rearrange("p t m j -> p (t m j)"),
+            )
+        cand_words = pick("cand_words", table_words[:].bitcast(U32), U32, cand_sb, tag="w1_grouped")
+        gs_row = gain_row("gs_row", gs_sb, 4, "w1_raw0")
+        gn_row = gain_row("gn_row", gn_sb, 5, "w1_raw1")
+
+        y, y_twin = [], []
+        for t in range(PACK):
+            y_bank = bank(f"y_bank{t}", t)
+            product(nc, y_bank, (w1_codes, w1_scales), t, (token_words, token_scales))
+            y_t = keep.tile([P, WINDOW], F32, name=f"y{t}")
+            twin = keep.tile([P, S], F32, name=f"y_twin{t}")
+            nc.scalar.activation(y_t[:, :S], y_bank[:], COPY)
+            nc.sync.dma_start(twin[:], y_t[:, :S])
+            y.append(y_t)
+            y_twin.append(twin)
+
         n2_sb = load_list("n2_sb", n2)
         n3_sb = load_list("n3_sb", n3)
         n6_sb = load_list("n6_sb", n6)
         n7_sb = load_list("n7_sb", n7)
 
-        def pick_columns(name, offsets):
-            words = keep.tile([P, S], U32, name=name + "_words", align_bytes=64)
-            scales = keep.tile([P, S], U8, name=name + "_scales", align_bytes=64)
-            nc.vector.tensor_copy(scales[:], table_scales[:].indirect(offsets[:]))
-            nc.vector.tensor_copy(words[:], table_words[:].bitcast(U32).indirect(offsets[:]))
-            return words, scales
-
-        token_words, token_scales = pick_columns("token", offs_sb)
-
-        w1_grouped = keep.tile([P, PACK, P, PACK], BF16, name="w1_grouped", align_bytes=64)
-        w1_codes = keep.tile([P, H], U32, name="w1_codes", align_bytes=64)
-        w1_scales = keep.tile([P, H], U8, name="w1_scales", align_bytes=64)
-        for u, copy in enumerate((nc.scalar.copy, nc.vector.tensor_copy)):
-            copy(
-                w1_grouped[:, :, u * (P // 2) : (u + 1) * (P // 2), :].rearrange("p t m j -> p m j t"),
-                w1_raw[u][:].rearrange("p j (m t) -> p m j t", t=PACK),
-            )
-        for t in range(PACK):
-            cols = slice(t * P, (t + 1) * P)
-            nc.vector.quantize_mx(
-                w1_codes[:, cols].bitcast(FP8X4), w1_scales[:, cols], w1_grouped[:, t].rearrange("p m j -> p (m j)")
-            )
-        cand_words, cand_scales = pick_columns("cand", cand_sb)
-
-        d4 = keep.tile([P, PACK, S], F32, name="d4")
-        d5 = keep.tile([P, PACK, S], F32, name="d5")
-        p1 = keep.tile([P, PACK, S], F32, name="p1")
-        p3 = keep.tile([P, PACK, S], F32, name="p3")
-        y, y_gn, at_n2 = [], [], []
-        for t in range(PACK):
-            bank = psum.tile([P, S], F32, name=f"y_bank{t}", tag=f"low{t}")
-            product(nc, bank, w1_codes, w1_scales, t, token_words, token_scales)
-            y_t = keep.tile([P, S], F32, name=f"y{t}")
-            y_gs_t = keep.tile([P, S], F32, name=f"y_gs{t}")
-            y_gn_t = keep.tile([P, S], F32, name=f"y_gn{t}")
-            at_n4 = ring.tile([P, S], F32, name="at_n4")
-            at_n5 = ring.tile([P, S], F32, name="at_n5")
-            nc.scalar.activation(y_t[:], bank[:], COPY)
-            nc.scalar.activation(y_gs_t[:], bank[:], COPY, scale=gs_sb[:, t : t + 1])
-            nc.vector.tensor_scalar(y_gn_t[:], y_t[:], gn_sb[:, t : t + 1], None, MULT)
-            gather_scalar(nc, at_n4, y_t, n4_sb)
-            gather_scalar(nc, at_n5, y_gs_t, n5_sb)
-            gather_fused(nc, p1[:, t], y_t, n1_sb, y_gn_t, MULT)
-            nc.vector.tensor_tensor(d4[:, t], at_n4[:], y_t[:], SUBTRACT)
-            nc.vector.tensor_tensor(d5[:, t], at_n5[:], y_gs_t[:], SUBTRACT)
-            y.append(y_t)
-            y_gn.append(y_gn_t)
-            at_n2.append(keep.tile([P, S], F32, name=f"at_n2_{t}"))
-
         w2_grouped = keep.tile([P, N, PACK], BF16, name="w2_grouped", align_bytes=64)
         w2_codes = keep.tile([P, N], U32, name="w2_codes", align_bytes=64)
         w2_scales = keep.tile([P, N], U8, name="w2_scales", align_bytes=64)
-        nc.vector.tensor_copy(
-            w2_grouped[:].rearrange("p (c i) j -> p c j i", i=4), w2_raw[:].rearrange("p j (c i) -> p c j i", i=4)
-        )
-        for t in range(N2_TILES_ON_VECTOR):
-            gather_vector(nc, at_n2[t], y_gn[t], n2_sb)
-        nc.vector.quantize_mx(w2_codes[:].bitcast(FP8X4), w2_scales[:], w2_grouped[:].rearrange("p c j -> p (c j)"))
 
-        z2_codes, z2_scales = combine_and_quantize(nc, keep, "z2", d4, d5, MULT)
+        p1 = []
+
+        def first_products(count):
+            for t in range(len(p1), len(p1) + count):
+                p1_t = keep.tile([P, S], F32, name=f"p1_{t}")
+                nc.vector.tensor_tensor(p1_t[:], y[t][:].indirect(n1_sb[:]), y_twin[t][:], MULT)
+                p1.append(p1_t)
+
+
+        for u in range(2):
+            d4 = [bank(f"d4_{u}{half}", (4 + half, half)[u]) for half in range(2)]
+            d5 = [bank(f"d5_{u}{half}", (6 + half, 2 + half)[u]) for half in range(2)]
+            for e in range(2):
+                t = 2 * u + e
+                minus_n4 = keep.tile([P, S], F32, name=f"minus_n4_{t}")
+                minus_n5 = keep.tile([P, S], F32, name=f"minus_n5_{t}")
+                if t < N5_TILES_ON_VECTOR:
+                    nc.vector.tensor_scalar(minus_n5[:], y[t][:].indirect(n5_sb[:]), -1.0, 0.0, MULT, ADD)
+                else:
+                    nc.scalar.activation(minus_n5[:], y[t][:].indirect(n5_sb[:]), COPY, scale=-1.0)
+                nc.scalar.activation(minus_n4[:], y[t][:].indirect(n4_sb[:]), COPY, scale=-1.0)
+                turned_sum(d5, e, y[t], minus_n5)
+                turned_sum(d4, e, y[t], minus_n4)
+            if u == 0:
+                nc.vector.tensor_copy(
+                    w2_grouped[:].rearrange("p (c i) j -> p c j i", i=4), w2_raw[:].rearrange("p j (c i) -> p c j i", i=4)
+                )
+            first_products((4, 0)[u])
+            if u == 0:
+                nc.vector.quantize_mx(w2_codes[:].bitcast(FP8X4), w2_scales[:], w2_grouped[:].rearrange("p c j -> p (c j)"))
+            scaled = [keep.tile([P, 2, P, 2], F32, name=f"scaled{u}{half}", align_bytes=64) for half in range(2)]
+            for half in range(2):
+                nc.vector.tensor_tensor(scaled[half][:], pairs(d5[half]), spread_row(gs_row, u), MULT)
+            rounded = [keep.tile([P, 2, P, 2], BF16, name=f"z2_rounded{u}{half}") for half in range(2)]
+            for half in range(2):
+                nc.vector.tensor_tensor(rounded[half][:], pairs(d4[half]), scaled[half][:], MULT)
+            if u == 0:
+                z2_back = [bank(f"z2_back{half}", 6 + half) for half in range(2)]
+            for half in range(2):
+                turn_back(z2_back[half], u, rounded[half])
+
+        z2 = quantize_halves("z2", z2_back)
         b_banks = []
         for m in range(C // P):
-            bank = psum.tile([P, S], F32, name=f"b_bank{m}")
-            product(nc, bank, cand_words, cand_scales, m, z2_codes, z2_scales)
-            b_banks.append(bank)
+            b_bank = bank(f"b_bank{m}", (4, 5, 2, 3)[m])
+            product(nc, b_bank, (cand_words, cand_scales), m, z2)
+            b_banks.append(b_bank)
 
-        for t in range(PACK):
-            if t >= N2_TILES_ON_VECTOR:
-                gather_scalar(nc, at_n2[t], y_gn[t], n2_sb)
-            gather_fused(nc, p3[:, t], y[t], n3_sb, at_n2[t], MULT)
-        z_codes, z_scales = combine_and_quantize(nc, keep, "z", p1, p3, ADD)
+        first_products(PACK - len(p1))
+        z_rounded = []
+        for u in range(2):
+            total = [bank(f"total{u}{half}", (half, 6 + half)[u]) for half in range(2)]
+            for e in range(2):
+                t = 2 * u + e
+                at_n2 = keep.tile([P, S], F32, name=f"at_n2_{t}", tag=(f"at_n2_{t}", f"z2_rounded1{e}")[u])
+                p3_t = keep.tile([P, S], F32, name=f"p3_{t}", tag=("scaled10", "z2_grouped1", "p3_2", "p3_3")[t], align_bytes=64)
+                nc.scalar.activation(at_n2[:], y[t][:].indirect(n2_sb[:]), COPY)
+                nc.vector.tensor_tensor(p3_t[:], y[t][:].indirect(n3_sb[:]), at_n2[:], MULT)
+                turned_sum(total, e, p1[t], p3_t)
+            rounded = [keep.tile([P, 2, P, 2], BF16, name=f"z_rounded{u}{half}") for half in range(2)]
+            for half in range(2):
+                nc.vector.tensor_tensor(rounded[half][:], pairs(total[half]), spread_row(gn_row, u), MULT)
+            z_rounded.append(rounded)
 
-        for m in range(N // P):
-            a_bank = psum.tile([P, S], F32, name=f"a_bank{m}", tag=f"low{m}")
-            product(nc, a_bank, w2_codes, w2_scales, m, z_codes, z_scales)
-            b_m = keep.tile([P, S], F32, name=f"b{m}")
+        def gap_of(m):
+            b_m = keep.tile([P, WINDOW], F32, name=f"b{m}")
             at_n6 = keep.tile([P, S], F32, name=f"at_n6_{m}")
             gap = keep.tile([P, S], F32, name=f"gap{m}")
-            gate = keep.tile([P, S], F32, name=f"gate{m}")
-            result = keep.tile([P, S], F32, name=f"result{m}")
-            nc.scalar.activation(b_m[:], b_banks[m][:], COPY)
-            gather_scalar(nc, at_n6, b_m, n6_sb)
-            if m < N7_TILES_ON_SCALAR:
+            nc.scalar.activation(b_m[:, :S], b_banks[m][:], COPY)
+            nc.scalar.activation(at_n6[:], b_m[:].indirect(n6_sb[:]), COPY)
+            if m >= C // P - N7_TILES_ON_SCALAR:
                 at_n7 = keep.tile([P, S], F32, name=f"at_n7_{m}")
-                gather_scalar(nc, at_n7, b_m, n7_sb)
+                nc.scalar.activation(at_n7[:], b_m[:].indirect(n7_sb[:]), COPY)
                 nc.vector.tensor_tensor(gap[:], at_n7[:], at_n6[:], SUBTRACT)
             else:
-                gather_fused(nc, gap, b_m, n7_sb, at_n6, SUBTRACT)
+                nc.vector.tensor_tensor(gap[:], b_m[:].indirect(n7_sb[:]), at_n6[:], SUBTRACT)
+            return gap
+
+        def finish(m, gap):
+            a_bank = bank(f"a_bank{m}", (0, 1, 6, 7)[m])
+            product(nc, a_bank, (w2_codes, w2_scales), m, z)
+            gate = keep.tile([P, S], F32, name=f"gate{m}")
+            result = keep.tile([P, S], F32, name=f"result{m}")
             nc.scalar.activation(gate[:], gap[:], TANH, scale=-0.0625)
             nc.vector.tensor_tensor(result[:], a_bank[:], gate[:], MULT)
             nc.sync.dma_start(out[m * P : (m + 1) * P, :], result[:])
+
+        gaps = [gap_of(0), gap_of(1)]
+        z_back = [bank(f"z_back{half}", 4 + half) for half in range(2)]
+        for u in range(2):
+            for half in range(2):
+                turn_back(z_back[half], u, z_rounded[u][half])
+        z = quantize_halves("z", z_back)
+        gaps.append(gap_of(2))
+        finish(0, gaps[0])
+        gaps.append(gap_of(3))
+        finish(1, gaps[1])
+        finish(2, gaps[2])
+        finish(3, gaps[3])

@@ -24,8 +24,11 @@ PACK = 4
 BANK = 512
 WINDOW = 2 * S
 LIST_GROUP = 16
+Y_GN_TILES_ON_SCALAR = 0
+N7_TILES_ON_SCALAR = 1
+N2_TILES_ON_VECTOR = 0
 N5_TILES_ON_VECTOR = 1
-N7_TILES_ON_SCALAR = 0
+HALVES = (slice(0, S // 2), slice(S // 2, S))
 
 
 def product(nc, bank, left, t, right):
@@ -59,8 +62,27 @@ def tile_picked_fkcdjointbdotquad_none_p_kernel(
 
         def load_gain(name, source):
             gain = keep.tile([P, PACK], F32, name=name)
-            nc.gpsimd.dma_start(gain[:], source.rearrange("(p t) o -> p (t o)", t=PACK))
+            raw = keep.tile([P, PACK], F32, name=name + "_raw")
+            nc.sync.dma_start(raw[:], source.rearrange("(p t) o -> p (t o)", t=PACK))
+            nc.gpsimd.tensor_scalar(gain[:], raw[:], 0.75, 0.0, MULT, ADD)
             return gain
+
+        def combine_and_quantize(name, left, right, op):
+            codes = keep.tile([P, S], U32, name=name + "_codes", align_bytes=64)
+            scales = keep.tile([P, S], U8, name=name + "_scales", align_bytes=64)
+            grouped = [keep.tile([P, S // 2, PACK], BF16, name=f"{name}_grouped{h}", align_bytes=64) for h in range(2)]
+            for half, cols in zip(grouped, HALVES):
+                nc.vector.tensor_tensor(
+                    half[:].rearrange("p (c i) t -> p c t i", i=4),
+                    left[:, :, cols].rearrange("p t (c i) -> p c t i", i=4),
+                    right[:, :, cols].rearrange("p t (c i) -> p c t i", i=4),
+                    op,
+                )
+            for half, cols in zip(grouped, HALVES):
+                nc.vector.quantize_mx(
+                    codes[:, cols].bitcast(FP8X4), scales[:, cols], half[:].rearrange("p j t -> p (j t)")
+                )
+            return codes, scales
 
         def turn(dst, src, start=True, stop=True):
             nc.tensor.matmul(dst, src, identity[:], start=start, stop=stop, is_transpose=True)
@@ -72,6 +94,13 @@ def tile_picked_fkcdjointbdotquad_none_p_kernel(
             row = keep.tile([P, 2, P, 2], F32, name=name, tag=tag)
             nc.scalar.activation(row[:], spread[:].rearrange("j (u e p) -> j u p e", u=2, e=2), COPY, scale=0.75)
             return row
+
+        def turn_tile(banks, e, source, start=False, stop=False):
+            for half in range(2):
+                for b in range(2):
+                    cols = slice((2 * half + b) * P, (2 * half + b + 1) * P)
+                    dst = banks[half][:, (2 * b + e) * P : (2 * b + e + 1) * P]
+                    turn(dst, source[:, cols], start=start and b == 0, stop=stop and b == 1)
 
         def turned_sum(banks, e, left, right):
             for half in range(2):
@@ -104,13 +133,15 @@ def tile_picked_fkcdjointbdotquad_none_p_kernel(
                 )
             return codes, scales
 
+
+        offs_sb = load_list("offs_sb", offs)
+        cand_sb = load_list("cand_sb", cand)
         table_scales = keep.tile([P, T], U8, name="table_scales")
-        nc.vector.memset(table_scales[:].bitcast(I32), 0)
+        nc.gpsimd.memset(table_scales[:].bitcast(I32), 0)
         for q in range(4):
-            nc.scalar.dma_start(
+            nc.sync.dma_start(
                 table_scales[32 * q : 32 * q + 4, :].bitcast(I32), x_scales[0, 4 * q : 4 * q + 4, :].bitcast(I32)
             )
-        offs_sb = load_list("offs_sb", offs)
         table_words = keep.tile([P, T], I32, name="table_words")
         nc.sync.dma_start(table_words[:], x_words[0].rearrange("p n t -> p (n t)").bitcast(I32))
         w1_rows = w1.rearrange("(p j) c -> p j c", j=PACK)
@@ -119,14 +150,22 @@ def tile_picked_fkcdjointbdotquad_none_p_kernel(
             part = keep.tile([P, PACK, H // 2], F32, name=f"w1_raw{u}")
             nc.sync.dma_start(part[:], w1_rows[:, :, u * (H // 2) : (u + 1) * (H // 2)])
             w1_raw.append(part)
-        gs_sb = load_gain("gs_sb", gs)
         gn_sb = load_gain("gn_sb", gn)
-        cand_sb = load_list("cand_sb", cand)
+        gs_sb = keep.tile([P, PACK], F32, name="gs_sb")
+        nc.sync.dma_start(gs_sb[:], gs.rearrange("(p t) o -> p (t o)", t=PACK))
+        w2_rows = w2.rearrange("(p j) c -> p j c", j=PACK)
+        w2_raw0 = keep.tile([P, PACK, N // 2], F32, name="w2_raw0")
+        nc.sync.dma_start(w2_raw0[:], w2_rows[:, :, HALVES[0]])
+        w2_raw1 = keep.tile([P, PACK, N // 2], F32, name="w2_raw1")
+        nc.sync.dma_start(w2_raw1[:], w2_rows[:, :, HALVES[1]])
         n5_sb = load_list("n5_sb", n5)
         n4_sb = load_list("n4_sb", n4)
-        w2_raw = keep.tile([P, PACK, N], F32, name="w2_raw")
-        nc.sync.dma_start(w2_raw[:], w2.rearrange("(p j) c -> p j c", j=PACK))
         n1_sb = load_list("n1_sb", n1)
+        n2_sb = load_list("n2_sb", n2)
+        n3_sb = load_list("n3_sb", n3)
+        n6_sb = load_list("n6_sb", n6)
+        n7_sb = load_list("n7_sb", n7)
+
         identity = keep.tile([P, P], F32, name="identity")
         make_identity(nc, identity[:])
 
@@ -136,8 +175,6 @@ def tile_picked_fkcdjointbdotquad_none_p_kernel(
             return picked
 
         token_scales = pick("token_scales", table_scales[:], U8, offs_sb)
-        token_words = pick("token_words", table_words[:].bitcast(U32), U32, offs_sb)
-        cand_scales = pick("cand_scales", table_scales[:], U8, cand_sb)
 
         w1_grouped = keep.tile([P, PACK, P, PACK], BF16, name="w1_grouped", align_bytes=64)
         w1_codes = keep.tile([P, H], U32, name="w1_codes", align_bytes=64)
@@ -158,42 +195,45 @@ def tile_picked_fkcdjointbdotquad_none_p_kernel(
                 w1_scales[:, cols],
                 w1_grouped[:, t : t + 2].rearrange("p t m j -> p (t m j)"),
             )
-        cand_words = pick("cand_words", table_words[:].bitcast(U32), U32, cand_sb, tag="w1_grouped")
-        gs_row = gain_row("gs_row", gs_sb, 4, "w1_raw0")
-        gn_row = gain_row("gn_row", gn_sb, 5, "w1_raw1")
+        token_words = pick("token_words", table_words[:].bitcast(U32), U32, offs_sb)
+        cand_scales = pick("cand_scales", table_scales[:], U8, cand_sb)
+        cand_words = pick("cand_words", table_words[:].bitcast(U32), U32, cand_sb)
 
-        y, y_twin = [], []
+        w2_grouped = keep.tile([P, N, PACK], BF16, name="w2_grouped", tag="w1_grouped", align_bytes=64)
+        w2_codes = keep.tile([P, N], U32, name="w2_codes", align_bytes=64)
+        w2_scales = keep.tile([P, N], U8, name="w2_scales", align_bytes=64)
+
+        for cols, raw in zip(HALVES, (w2_raw0, w2_raw1)):
+            nc.vector.tensor_copy(
+                w2_grouped[:, cols].rearrange("p (c i) j -> p c j i", i=4),
+                raw[:].rearrange("p j (c i) -> p c j i", i=4),
+            )
+        gs_row = gain_row("gs_row", gs_sb, 4, "w1_raw1")
+        p1 = keep.tile([P, PACK, S], F32, name="p1")
+        y, y_gn = [], []
         for t in range(PACK):
             y_bank = bank(f"y_bank{t}", t)
             product(nc, y_bank, (w1_codes, w1_scales), t, (token_words, token_scales))
             y_t = keep.tile([P, WINDOW], F32, name=f"y{t}")
-            twin = keep.tile([P, S], F32, name=f"y_twin{t}")
+            y_gn_t = keep.tile([P, WINDOW], F32, name=f"y_gn{t}")
             nc.scalar.activation(y_t[:, :S], y_bank[:], COPY)
-            nc.sync.dma_start(twin[:], y_t[:, :S])
+            if t >= PACK - Y_GN_TILES_ON_SCALAR:
+                nc.scalar.activation(y_gn_t[:, :S], y_bank[:], COPY, scale=gn_sb[:, t : t + 1])
+            else:
+                nc.vector.tensor_scalar(y_gn_t[:, :S], y_t[:, :S], gn_sb[:, t : t + 1], None, MULT)
             y.append(y_t)
-            y_twin.append(twin)
+            y_gn.append(y_gn_t)
 
-        n2_sb = load_list("n2_sb", n2)
-        n3_sb = load_list("n3_sb", n3)
-        n6_sb = load_list("n6_sb", n6)
-        n7_sb = load_list("n7_sb", n7)
+        def first_product(t):
+            nc.vector.tensor_tensor(p1[:, t], y[t][:].indirect(n1_sb[:]), y_gn[t][:, :S], MULT)
 
-        w2_grouped = keep.tile([P, N, PACK], BF16, name="w2_grouped", align_bytes=64)
-        w2_codes = keep.tile([P, N], U32, name="w2_codes", align_bytes=64)
-        w2_scales = keep.tile([P, N], U8, name="w2_scales", align_bytes=64)
-
-        p1 = []
-
-        def first_products(count):
-            for t in range(len(p1), len(p1) + count):
-                p1_t = keep.tile([P, S], F32, name=f"p1_{t}")
-                nc.vector.tensor_tensor(p1_t[:], y[t][:].indirect(n1_sb[:]), y_twin[t][:], MULT)
-                p1.append(p1_t)
-
-
+        z2_rounded = []
         for u in range(2):
             d4 = [bank(f"d4_{u}{half}", (4 + half, half)[u]) for half in range(2)]
             d5 = [bank(f"d5_{u}{half}", (6 + half, 2 + half)[u]) for half in range(2)]
+            for e in range(2):
+                turn_tile(d5, e, y[2 * u + e], start=e == 0)
+                turn_tile(d4, e, y[2 * u + e], start=e == 0)
             for e in range(2):
                 t = 2 * u + e
                 minus_n4 = keep.tile([P, S], F32, name=f"minus_n4_{t}")
@@ -203,25 +243,25 @@ def tile_picked_fkcdjointbdotquad_none_p_kernel(
                 else:
                     nc.scalar.activation(minus_n5[:], y[t][:].indirect(n5_sb[:]), COPY, scale=-1.0)
                 nc.scalar.activation(minus_n4[:], y[t][:].indirect(n4_sb[:]), COPY, scale=-1.0)
-                turned_sum(d5, e, y[t], minus_n5)
-                turned_sum(d4, e, y[t], minus_n4)
+                turn_tile(d5, e, minus_n5, stop=e == 1)
+                turn_tile(d4, e, minus_n4, stop=e == 1)
+            for t in (range(4), range(4, PACK))[u]:
+                first_product(t)
             if u == 0:
-                nc.vector.tensor_copy(
-                    w2_grouped[:].rearrange("p (c i) j -> p c j i", i=4), w2_raw[:].rearrange("p j (c i) -> p c j i", i=4)
+                nc.vector.quantize_mx(
+                    w2_codes[:].bitcast(FP8X4), w2_scales[:], w2_grouped[:].rearrange("p c j -> p (c j)")
                 )
-            first_products((4, 0)[u])
-            if u == 0:
-                nc.vector.quantize_mx(w2_codes[:].bitcast(FP8X4), w2_scales[:], w2_grouped[:].rearrange("p c j -> p (c j)"))
             scaled = [keep.tile([P, 2, P, 2], F32, name=f"scaled{u}{half}", align_bytes=64) for half in range(2)]
             for half in range(2):
                 nc.vector.tensor_tensor(scaled[half][:], pairs(d5[half]), spread_row(gs_row, u), MULT)
             rounded = [keep.tile([P, 2, P, 2], BF16, name=f"z2_rounded{u}{half}") for half in range(2)]
             for half in range(2):
                 nc.vector.tensor_tensor(rounded[half][:], pairs(d4[half]), scaled[half][:], MULT)
-            if u == 0:
-                z2_back = [bank(f"z2_back{half}", 6 + half) for half in range(2)]
+            z2_rounded.append(rounded)
+        z2_back = [bank(f"z2_back{half}", 6 + half) for half in range(2)]
+        for u in range(2):
             for half in range(2):
-                turn_back(z2_back[half], u, rounded[half])
+                turn_back(z2_back[half], u, z2_rounded[u][half])
 
         z2 = quantize_halves("z2", z2_back)
         b_banks = []
@@ -230,21 +270,14 @@ def tile_picked_fkcdjointbdotquad_none_p_kernel(
             product(nc, b_bank, (cand_words, cand_scales), m, z2)
             b_banks.append(b_bank)
 
-        first_products(PACK - len(p1))
-        z_rounded = []
-        for u in range(2):
-            total = [bank(f"total{u}{half}", (half, 6 + half)[u]) for half in range(2)]
-            for e in range(2):
-                t = 2 * u + e
-                at_n2 = keep.tile([P, S], F32, name=f"at_n2_{t}", tag=(f"at_n2_{t}", f"z2_rounded1{e}")[u])
-                p3_t = keep.tile([P, S], F32, name=f"p3_{t}", tag=("scaled10", "z2_grouped1", "p3_2", "p3_3")[t], align_bytes=64)
-                nc.scalar.activation(at_n2[:], y[t][:].indirect(n2_sb[:]), COPY)
-                nc.vector.tensor_tensor(p3_t[:], y[t][:].indirect(n3_sb[:]), at_n2[:], MULT)
-                turned_sum(total, e, p1[t], p3_t)
-            rounded = [keep.tile([P, 2, P, 2], BF16, name=f"z_rounded{u}{half}") for half in range(2)]
-            for half in range(2):
-                nc.vector.tensor_tensor(rounded[half][:], pairs(total[half]), spread_row(gn_row, u), MULT)
-            z_rounded.append(rounded)
+        p3 = keep.tile([P, PACK, S], F32, name="p3", tag="scaled10", align_bytes=64)
+        for t in range(PACK):
+            at_n2 = keep.tile([P, S], F32, name=f"at_n2_{t}", tag=("at_n2_0", "at_n2_1", "z2_rounded10", "z2_rounded11")[t])
+            if t < N2_TILES_ON_VECTOR:
+                nc.vector.tensor_copy(at_n2[:], y_gn[t][:].indirect(n2_sb[:]))
+            else:
+                nc.scalar.activation(at_n2[:], y_gn[t][:].indirect(n2_sb[:]), COPY)
+            nc.vector.tensor_tensor(p3[:, t], y[t][:].indirect(n3_sb[:]), at_n2[:], MULT)
 
         def gap_of(m):
             b_m = keep.tile([P, WINDOW], F32, name=f"b{m}")
@@ -265,19 +298,12 @@ def tile_picked_fkcdjointbdotquad_none_p_kernel(
             product(nc, a_bank, (w2_codes, w2_scales), m, z)
             gate = keep.tile([P, S], F32, name=f"gate{m}")
             result = keep.tile([P, S], F32, name=f"result{m}")
-            nc.scalar.activation(gate[:], gap[:], TANH, scale=-0.0625)
-            nc.vector.tensor_tensor(result[:], a_bank[:], gate[:], MULT)
-            nc.sync.dma_start(out[m * P : (m + 1) * P, :], result[:])
+            for cols in HALVES if m == N // P - 1 else (slice(0, S),):
+                nc.scalar.activation(gate[:, cols], gap[:, cols], TANH, scale=-0.0625)
+                nc.vector.tensor_tensor(result[:, cols], a_bank[:, cols], gate[:, cols], MULT)
+                nc.sync.dma_start(out[m * P : (m + 1) * P, cols], result[:, cols])
 
-        gaps = [gap_of(0), gap_of(1)]
-        z_back = [bank(f"z_back{half}", 4 + half) for half in range(2)]
-        for u in range(2):
-            for half in range(2):
-                turn_back(z_back[half], u, z_rounded[u][half])
-        z = quantize_halves("z", z_back)
-        gaps.append(gap_of(2))
-        finish(0, gaps[0])
-        gaps.append(gap_of(3))
-        finish(1, gaps[1])
-        finish(2, gaps[2])
-        finish(3, gaps[3])
+        z = combine_and_quantize("z", p1, p3, ADD)
+        gaps = [gap_of(m) for m in range(C // P)]
+        for m in range(N // P):
+            finish(m, gaps[m])

@@ -22,17 +22,18 @@ TANH = mybir.ActivationFunctionType.Tanh
 P = 128
 PACK = 4
 BANK = 512
-WINDOW = 2 * S
 LIST_GROUP = 16
-Y_GN_TILES_ON_SCALAR = 0
-N7_TILES_ON_SCALAR = 1
-N2_TILES_ON_VECTOR = 0
-N5_TILES_ON_VECTOR = 1
+QUADRANT = 32
+LINE = 4
 HALVES = (slice(0, S // 2), slice(S // 2, S))
+WINDOW = 2 * S
+N5_TILE_ON_VECTOR = 0
+N7_TILE_ON_SCALAR = 3
+W1_SCALAR_ROWS = 32
 
 
-def product(nc, bank, left, t, right):
-    cols = slice(t * P, (t + 1) * P)
+def product(nc, bank, left, tile, right):
+    cols = slice(tile * P, (tile + 1) * P)
     nc.tensor.matmul_mx(
         out=bank[:],
         lhsT=left[0][:, cols].bitcast(FP8X4),
@@ -42,6 +43,14 @@ def product(nc, bank, left, t, right):
         start=True,
         stop=True,
     )
+
+
+def interleaved(grouped, run):
+    return grouped.rearrange("p (c i) t -> p c t i", i=run)
+
+
+def by_rows(rows, run):
+    return rows.rearrange("p t (c i) -> p c t i", i=run)
 
 
 def tile_picked_fkcdjointbdotquad_none_p_kernel(
@@ -62,102 +71,31 @@ def tile_picked_fkcdjointbdotquad_none_p_kernel(
 
         def load_gain(name, source):
             gain = keep.tile([P, PACK], F32, name=name)
-            raw = keep.tile([P, PACK], F32, name=name + "_raw")
-            nc.sync.dma_start(raw[:], source.rearrange("(p t) o -> p (t o)", t=PACK))
-            nc.gpsimd.tensor_scalar(gain[:], raw[:], 0.75, 0.0, MULT, ADD)
+            nc.sync.dma_start(gain[:], source.rearrange("(p t) o -> p (t o)", t=PACK))
             return gain
 
-        def combine_and_quantize(name, left, right, op):
-            codes = keep.tile([P, S], U32, name=name + "_codes", align_bytes=64)
-            scales = keep.tile([P, S], U8, name=name + "_scales", align_bytes=64)
-            grouped = [keep.tile([P, S // 2, PACK], BF16, name=f"{name}_grouped{h}", align_bytes=64) for h in range(2)]
-            for half, cols in zip(grouped, HALVES):
-                nc.vector.tensor_tensor(
-                    half[:].rearrange("p (c i) t -> p c t i", i=4),
-                    left[:, :, cols].rearrange("p t (c i) -> p c t i", i=4),
-                    right[:, :, cols].rearrange("p t (c i) -> p c t i", i=4),
-                    op,
-                )
-            for half, cols in zip(grouped, HALVES):
-                nc.vector.quantize_mx(
-                    codes[:, cols].bitcast(FP8X4), scales[:, cols], half[:].rearrange("p j t -> p (j t)")
-                )
-            return codes, scales
-
-        def turn(dst, src, start=True, stop=True):
-            nc.tensor.matmul(dst, src, identity[:], start=start, stop=stop, is_transpose=True)
-
-        def gain_row(name, gain, number, tag):
-            spread = bank(name + "_bank", number)
-            for t in range(PACK):
-                turn(spread[:, t * P : (t + 1) * P], gain[:, t : t + 1].to_broadcast([P, P]))
-            row = keep.tile([P, 2, P, 2], F32, name=name, tag=tag)
-            nc.scalar.activation(row[:], spread[:].rearrange("j (u e p) -> j u p e", u=2, e=2), COPY, scale=0.75)
-            return row
-
-        def turn_tile(banks, e, source, start=False, stop=False):
-            for half in range(2):
-                for b in range(2):
-                    cols = slice((2 * half + b) * P, (2 * half + b + 1) * P)
-                    dst = banks[half][:, (2 * b + e) * P : (2 * b + e + 1) * P]
-                    turn(dst, source[:, cols], start=start and b == 0, stop=stop and b == 1)
-
-        def turned_sum(banks, e, left, right):
-            for half in range(2):
-                for b in range(2):
-                    cols = slice((2 * half + b) * P, (2 * half + b + 1) * P)
-                    dst = banks[half][:, (2 * b + e) * P : (2 * b + e + 1) * P]
-                    turn(dst, left[:, cols], start=True, stop=False)
-                    turn(dst, right[:, cols], start=False, stop=True)
-
-        def pairs(turned):
-            return turned[:].rearrange("j (b e p) -> j b p e", b=2, e=2)
-
-        def spread_row(row, u):
-            return row[:, u].unsqueeze(1).to_broadcast([P, 2, P, 2])
-
-        def turn_back(back, u, rounded):
-            words = rounded[:].rearrange("j b p e -> j (b p e)").bitcast(F32)
-            for b in range(2):
-                turn(back[:, (2 * u + b) * P : (2 * u + b + 1) * P], words[:, b * P : (b + 1) * P])
-
-        def quantize_halves(name, backs):
-            codes = keep.tile([P, S], U32, name=name + "_codes", align_bytes=64)
-            scales = keep.tile([P, S], U8, name=name + "_scales", align_bytes=64)
-            for half in range(2):
-                cols = slice(half * (S // 2), (half + 1) * (S // 2))
-                grouped = keep.tile([P, S // 2, PACK], BF16, name=f"{name}_grouped{half}", align_bytes=64)
-                nc.scalar.copy(grouped[:].bitcast(F32), backs[half][:].rearrange("p (u j) -> p j u", u=2))
-                nc.vector.quantize_mx(
-                    codes[:, cols].bitcast(FP8X4), scales[:, cols], grouped[:].rearrange("p j t -> p (j t)")
-                )
-            return codes, scales
-
+        def load_weight_half(name, source, cols):
+            half = keep.tile([P, PACK, S // 2], F32, name=name)
+            nc.sync.dma_start(half[:], source.rearrange("(p j) c -> p j c", j=PACK)[:, :, cols])
+            return half
 
         offs_sb = load_list("offs_sb", offs)
         cand_sb = load_list("cand_sb", cand)
         table_scales = keep.tile([P, T], U8, name="table_scales")
         nc.gpsimd.memset(table_scales[:].bitcast(I32), 0)
-        for q in range(4):
+        for q in range(P // QUADRANT):
             nc.sync.dma_start(
-                table_scales[32 * q : 32 * q + 4, :].bitcast(I32), x_scales[0, 4 * q : 4 * q + 4, :].bitcast(I32)
+                table_scales[QUADRANT * q : QUADRANT * q + 4, :].bitcast(I32),
+                x_scales[0, 4 * q : 4 * q + 4, :].bitcast(I32),
             )
         table_words = keep.tile([P, T], I32, name="table_words")
         nc.sync.dma_start(table_words[:], x_words[0].rearrange("p n t -> p (n t)").bitcast(I32))
-        w1_rows = w1.rearrange("(p j) c -> p j c", j=PACK)
-        w1_raw = []
-        for u in range(2):
-            part = keep.tile([P, PACK, H // 2], F32, name=f"w1_raw{u}")
-            nc.sync.dma_start(part[:], w1_rows[:, :, u * (H // 2) : (u + 1) * (H // 2)])
-            w1_raw.append(part)
-        gn_sb = load_gain("gn_sb", gn)
-        gs_sb = keep.tile([P, PACK], F32, name="gs_sb")
-        nc.sync.dma_start(gs_sb[:], gs.rearrange("(p t) o -> p (t o)", t=PACK))
-        w2_rows = w2.rearrange("(p j) c -> p j c", j=PACK)
-        w2_raw0 = keep.tile([P, PACK, N // 2], F32, name="w2_raw0")
-        nc.sync.dma_start(w2_raw0[:], w2_rows[:, :, HALVES[0]])
-        w2_raw1 = keep.tile([P, PACK, N // 2], F32, name="w2_raw1")
-        nc.sync.dma_start(w2_raw1[:], w2_rows[:, :, HALVES[1]])
+        w1_raw = [load_weight_half(f"w1_raw{h}", w1, HALVES[h]) for h in range(2)]
+        gn_sb = keep.tile([P, PACK], F32, name="gn_sb")
+        gn_raw = load_gain("gn_sb_raw", gn)
+        nc.gpsimd.tensor_scalar(gn_sb[:], gn_raw[:], 0.75, 0.0, MULT, ADD)
+        gs_sb = load_gain("gs_sb", gs)
+        w2_raw = [load_weight_half(f"w2_raw{h}", w2, HALVES[h]) for h in range(2)]
         n5_sb = load_list("n5_sb", n5)
         n4_sb = load_list("n4_sb", n4)
         n1_sb = load_list("n1_sb", n1)
@@ -165,28 +103,31 @@ def tile_picked_fkcdjointbdotquad_none_p_kernel(
         n3_sb = load_list("n3_sb", n3)
         n6_sb = load_list("n6_sb", n6)
         n7_sb = load_list("n7_sb", n7)
-
         identity = keep.tile([P, P], F32, name="identity")
         make_identity(nc, identity[:])
 
-        def pick(name, table, dtype, offsets, tag=None):
-            picked = keep.tile([P, S], dtype, name=name, tag=tag or name, align_bytes=64)
+        def pick(name, table, dtype, offsets):
+            picked = keep.tile([P, S], dtype, name=name, align_bytes=64)
             nc.vector.tensor_copy(picked[:], table.indirect(offsets[:]))
             return picked
+
+        def turn(dst, src, start=True, stop=True):
+            nc.tensor.matmul(dst, src, identity[:], start=start, stop=stop, is_transpose=True)
 
         token_scales = pick("token_scales", table_scales[:], U8, offs_sb)
 
         w1_grouped = keep.tile([P, PACK, P, PACK], BF16, name="w1_grouped", align_bytes=64)
         w1_codes = keep.tile([P, H], U32, name="w1_codes", align_bytes=64)
         w1_scales = keep.tile([P, H], U8, name="w1_scales", align_bytes=64)
-        for copy, u, first, last in (
-            (nc.scalar.copy, 0, 0, 64),
-            (nc.scalar.copy, 1, 0, 32),
-            (nc.vector.tensor_copy, 1, 32, 64),
+        rows_a_half = P // 2
+        for copy, h, first, last in (
+            (nc.scalar.copy, 0, 0, rows_a_half),
+            (nc.scalar.copy, 1, 0, W1_SCALAR_ROWS),
+            (nc.vector.tensor_copy, 1, W1_SCALAR_ROWS, rows_a_half),
         ):
             copy(
-                w1_grouped[:, :, 64 * u + first : 64 * u + last, :].rearrange("p t m j -> p m j t"),
-                w1_raw[u][:, :, PACK * first : PACK * last].rearrange("p j (m t) -> p m j t", t=PACK),
+                w1_grouped[:, :, rows_a_half * h + first : rows_a_half * h + last, :].rearrange("p t m j -> p m j t"),
+                w1_raw[h][:, :, PACK * first : PACK * last].rearrange("p j (m t) -> p m j t", t=PACK),
             )
         for t in (0, 2):
             cols = slice(t * P, (t + 2) * P)
@@ -202,13 +143,15 @@ def tile_picked_fkcdjointbdotquad_none_p_kernel(
         w2_grouped = keep.tile([P, N, PACK], BF16, name="w2_grouped", tag="w1_grouped", align_bytes=64)
         w2_codes = keep.tile([P, N], U32, name="w2_codes", align_bytes=64)
         w2_scales = keep.tile([P, N], U8, name="w2_scales", align_bytes=64)
+        for cols, raw in zip(HALVES, w2_raw):
+            nc.vector.tensor_copy(interleaved(w2_grouped[:, cols], LINE), by_rows(raw[:], LINE))
 
-        for cols, raw in zip(HALVES, (w2_raw0, w2_raw1)):
-            nc.vector.tensor_copy(
-                w2_grouped[:, cols].rearrange("p (c i) j -> p c j i", i=4),
-                raw[:].rearrange("p j (c i) -> p c j i", i=4),
-            )
-        gs_row = gain_row("gs_row", gs_sb, 4, "w1_raw1")
+        gs_bank = bank("gs_row_bank", 4)
+        for t in range(PACK):
+            turn(gs_bank[:, t * P : (t + 1) * P], gs_sb[:, t : t + 1].to_broadcast([P, P]))
+        gs_row = keep.tile([P, 2, P, 2], F32, name="gs_row", tag="w1_raw1")
+        nc.scalar.activation(gs_row[:], gs_bank[:].rearrange("j (u e p) -> j u p e", u=2, e=2), COPY, scale=0.75)
+
         p1 = keep.tile([P, PACK, S], F32, name="p1")
         y, y_gn = [], []
         for t in range(PACK):
@@ -217,20 +160,25 @@ def tile_picked_fkcdjointbdotquad_none_p_kernel(
             y_t = keep.tile([P, WINDOW], F32, name=f"y{t}")
             y_gn_t = keep.tile([P, WINDOW], F32, name=f"y_gn{t}")
             nc.scalar.activation(y_t[:, :S], y_bank[:], COPY)
-            if t >= PACK - Y_GN_TILES_ON_SCALAR:
-                nc.scalar.activation(y_gn_t[:, :S], y_bank[:], COPY, scale=gn_sb[:, t : t + 1])
-            else:
-                nc.vector.tensor_scalar(y_gn_t[:, :S], y_t[:, :S], gn_sb[:, t : t + 1], None, MULT)
+            nc.vector.tensor_scalar(y_gn_t[:, :S], y_t[:, :S], gn_sb[:, t : t + 1], None, MULT)
             y.append(y_t)
             y_gn.append(y_gn_t)
 
-        def first_product(t):
-            nc.vector.tensor_tensor(p1[:, t], y[t][:].indirect(n1_sb[:]), y_gn[t][:, :S], MULT)
+        def turn_tile(banks, e, source, start=False, stop=False):
+            for h in range(2):
+                for g in range(2):
+                    cols = slice((2 * h + g) * P, (2 * h + g + 1) * P)
+                    dst = banks[h][:, (2 * g + e) * P : (2 * g + e + 1) * P]
+                    turn(dst, source[:, cols], start=start and g == 0, stop=stop and g == 1)
+
+        def pairs(turned):
+            return turned[:].rearrange("j (g e p) -> j g p e", g=2, e=2)
 
         z2_rounded = []
         for u in range(2):
-            d4 = [bank(f"d4_{u}{half}", (4 + half, half)[u]) for half in range(2)]
-            d5 = [bank(f"d5_{u}{half}", (6 + half, 2 + half)[u]) for half in range(2)]
+            first_bank = (4, 0)[u]
+            d4 = [bank(f"d4_{u}{h}", first_bank + h) for h in range(2)]
+            d5 = [bank(f"d5_{u}{h}", first_bank + 2 + h) for h in range(2)]
             for e in range(2):
                 turn_tile(d5, e, y[2 * u + e], start=e == 0)
                 turn_tile(d4, e, y[2 * u + e], start=e == 0)
@@ -238,72 +186,87 @@ def tile_picked_fkcdjointbdotquad_none_p_kernel(
                 t = 2 * u + e
                 minus_n4 = keep.tile([P, S], F32, name=f"minus_n4_{t}")
                 minus_n5 = keep.tile([P, S], F32, name=f"minus_n5_{t}")
-                if t < N5_TILES_ON_VECTOR:
+                if t == N5_TILE_ON_VECTOR:
                     nc.vector.tensor_scalar(minus_n5[:], y[t][:].indirect(n5_sb[:]), -1.0, 0.0, MULT, ADD)
                 else:
                     nc.scalar.activation(minus_n5[:], y[t][:].indirect(n5_sb[:]), COPY, scale=-1.0)
                 nc.scalar.activation(minus_n4[:], y[t][:].indirect(n4_sb[:]), COPY, scale=-1.0)
                 turn_tile(d5, e, minus_n5, stop=e == 1)
                 turn_tile(d4, e, minus_n4, stop=e == 1)
-            for t in (range(4), range(4, PACK))[u]:
-                first_product(t)
             if u == 0:
+                for t in range(PACK):
+                    nc.vector.tensor_tensor(p1[:, t], y[t][:].indirect(n1_sb[:]), y_gn[t][:, :S], MULT)
                 nc.vector.quantize_mx(
                     w2_codes[:].bitcast(FP8X4), w2_scales[:], w2_grouped[:].rearrange("p c j -> p (c j)")
                 )
-            scaled = [keep.tile([P, 2, P, 2], F32, name=f"scaled{u}{half}", align_bytes=64) for half in range(2)]
-            for half in range(2):
-                nc.vector.tensor_tensor(scaled[half][:], pairs(d5[half]), spread_row(gs_row, u), MULT)
-            rounded = [keep.tile([P, 2, P, 2], BF16, name=f"z2_rounded{u}{half}") for half in range(2)]
-            for half in range(2):
-                nc.vector.tensor_tensor(rounded[half][:], pairs(d4[half]), scaled[half][:], MULT)
+            gs_pairs = gs_row[:, u].unsqueeze(1).to_broadcast([P, 2, P, 2])
+            scaled = [keep.tile([P, 2, P, 2], F32, name=f"scaled{u}{h}", align_bytes=64) for h in range(2)]
+            for h in range(2):
+                nc.vector.tensor_tensor(scaled[h][:], pairs(d5[h]), gs_pairs, MULT)
+            rounded = [keep.tile([P, 2, P, 2], BF16, name=f"z2_rounded{u}{h}") for h in range(2)]
+            for h in range(2):
+                nc.vector.tensor_tensor(rounded[h][:], pairs(d4[h]), scaled[h][:], MULT)
             z2_rounded.append(rounded)
-        z2_back = [bank(f"z2_back{half}", 6 + half) for half in range(2)]
-        for u in range(2):
-            for half in range(2):
-                turn_back(z2_back[half], u, z2_rounded[u][half])
 
-        z2 = quantize_halves("z2", z2_back)
+        z2_back = [bank(f"z2_back{h}", 6 + h) for h in range(2)]
+        for u in range(2):
+            for h in range(2):
+                as_f32 = z2_rounded[u][h][:].rearrange("j g p e -> j (g p e)").bitcast(F32)
+                for g in range(2):
+                    turn(z2_back[h][:, (2 * u + g) * P : (2 * u + g + 1) * P], as_f32[:, g * P : (g + 1) * P])
+        z2_codes = keep.tile([P, S], U32, name="z2_codes", align_bytes=64)
+        z2_scales = keep.tile([P, S], U8, name="z2_scales", align_bytes=64)
+        for h, cols in enumerate(HALVES):
+            grouped = keep.tile([P, S // 2, PACK], BF16, name=f"z2_grouped{h}", align_bytes=64)
+            nc.scalar.copy(grouped[:].bitcast(F32), z2_back[h][:].rearrange("p (u j) -> p j u", u=2))
+            nc.vector.quantize_mx(
+                z2_codes[:, cols].bitcast(FP8X4), z2_scales[:, cols], grouped[:].rearrange("p j t -> p (j t)")
+            )
+
         b_banks = []
-        for m in range(C // P):
-            b_bank = bank(f"b_bank{m}", (4, 5, 2, 3)[m])
-            product(nc, b_bank, (cand_words, cand_scales), m, z2)
+        for m, number in enumerate((4, 5, 2, 3)):
+            b_bank = bank(f"b_bank{m}", number)
+            product(nc, b_bank, (cand_words, cand_scales), m, (z2_codes, z2_scales))
             b_banks.append(b_bank)
 
         p3 = keep.tile([P, PACK, S], F32, name="p3", tag="scaled10", align_bytes=64)
-        for t in range(PACK):
-            at_n2 = keep.tile([P, S], F32, name=f"at_n2_{t}", tag=("at_n2_0", "at_n2_1", "z2_rounded10", "z2_rounded11")[t])
-            if t < N2_TILES_ON_VECTOR:
-                nc.vector.tensor_copy(at_n2[:], y_gn[t][:].indirect(n2_sb[:]))
-            else:
-                nc.scalar.activation(at_n2[:], y_gn[t][:].indirect(n2_sb[:]), COPY)
+        for t, tag in enumerate(("at_n2_0", "at_n2_1", "z2_rounded10", "z2_rounded11")):
+            at_n2 = keep.tile([P, S], F32, name=f"at_n2_{t}", tag=tag)
+            nc.scalar.activation(at_n2[:], y_gn[t][:].indirect(n2_sb[:]), COPY)
             nc.vector.tensor_tensor(p3[:, t], y[t][:].indirect(n3_sb[:]), at_n2[:], MULT)
+        z_codes = keep.tile([P, S], U32, name="z_codes", align_bytes=64)
+        z_scales = keep.tile([P, S], U8, name="z_scales", align_bytes=64)
+        z_grouped = [keep.tile([P, S // 2, PACK], BF16, name=f"z_grouped{h}", align_bytes=64) for h in range(2)]
+        for grouped, cols in zip(z_grouped, HALVES):
+            nc.vector.tensor_tensor(
+                interleaved(grouped[:], 2), by_rows(p1[:, :, cols], 2), by_rows(p3[:, :, cols], 2), ADD
+            )
+        for grouped, cols in zip(z_grouped, HALVES):
+            nc.vector.quantize_mx(
+                z_codes[:, cols].bitcast(FP8X4), z_scales[:, cols], grouped[:].rearrange("p j t -> p (j t)")
+            )
 
-        def gap_of(m):
+        gaps = []
+        for m in range(C // P):
             b_m = keep.tile([P, WINDOW], F32, name=f"b{m}")
             at_n6 = keep.tile([P, S], F32, name=f"at_n6_{m}")
             gap = keep.tile([P, S], F32, name=f"gap{m}")
             nc.scalar.activation(b_m[:, :S], b_banks[m][:], COPY)
             nc.scalar.activation(at_n6[:], b_m[:].indirect(n6_sb[:]), COPY)
-            if m >= C // P - N7_TILES_ON_SCALAR:
+            if m == N7_TILE_ON_SCALAR:
                 at_n7 = keep.tile([P, S], F32, name=f"at_n7_{m}")
                 nc.scalar.activation(at_n7[:], b_m[:].indirect(n7_sb[:]), COPY)
                 nc.vector.tensor_tensor(gap[:], at_n7[:], at_n6[:], SUBTRACT)
             else:
                 nc.vector.tensor_tensor(gap[:], b_m[:].indirect(n7_sb[:]), at_n6[:], SUBTRACT)
-            return gap
+            gaps.append(gap)
 
-        def finish(m, gap):
-            a_bank = bank(f"a_bank{m}", (0, 1, 6, 7)[m])
-            product(nc, a_bank, (w2_codes, w2_scales), m, z)
+        for m, number in enumerate((0, 1, 6, 7)):
+            a_bank = bank(f"a_bank{m}", number)
+            product(nc, a_bank, (w2_codes, w2_scales), m, (z_codes, z_scales))
             gate = keep.tile([P, S], F32, name=f"gate{m}")
             result = keep.tile([P, S], F32, name=f"result{m}")
             for cols in HALVES if m == N // P - 1 else (slice(0, S),):
-                nc.scalar.activation(gate[:, cols], gap[:, cols], TANH, scale=-0.0625)
+                nc.scalar.activation(gate[:, cols], gaps[m][:, cols], TANH, scale=-0.0625)
                 nc.vector.tensor_tensor(result[:, cols], a_bank[:, cols], gate[:, cols], MULT)
                 nc.sync.dma_start(out[m * P : (m + 1) * P, cols], result[:, cols])
-
-        z = combine_and_quantize("z", p1, p3, ADD)
-        gaps = [gap_of(m) for m in range(C // P)]
-        for m in range(N // P):
-            finish(m, gaps[m])

from contextlib import ExitStack

import concourse.mybir as mybir
from concourse.masks import make_identity

K, T, S, N, H, C = 512, 2048, 512, 512, 512, 512
FLOPS = 2 * (K * H * S + H * N * S + K * C * S)

F32 = mybir.dt.float32
BF16 = mybir.dt.bfloat16
I32 = mybir.dt.int32
U32 = mybir.dt.uint32
U16 = mybir.dt.uint16
U8 = mybir.dt.uint8
FP8X4 = mybir.dt.float8_e4m3fn_x4
MULT = mybir.AluOpType.mult
ADD = mybir.AluOpType.add
SUBTRACT = mybir.AluOpType.subtract
COPY = mybir.ActivationFunctionType.Copy
TANH = mybir.ActivationFunctionType.Tanh

P = 128
PACK = 4
BANK = 512
LIST_GROUP = 16
QUADRANT = 32
LINE = 4
HALVES = (slice(0, S // 2), slice(S // 2, S))
WINDOW = 2 * S
N5_TILE_ON_VECTOR = 0
N7_TILE_ON_SCALAR = 3
W1_SCALAR_ROWS = 32


def product(nc, bank, left, tile, right):
    cols = slice(tile * P, (tile + 1) * P)
    nc.tensor.matmul_mx(
        out=bank[:],
        lhsT=left[0][:, cols].bitcast(FP8X4),
        lhsT_scale=left[1][:, cols],
        rhs=right[0][:].bitcast(FP8X4),
        rhs_scale=right[1][:],
        start=True,
        stop=True,
    )


def interleaved(grouped, run):
    return grouped.rearrange("p (c i) t -> p c t i", i=run)


def by_rows(rows, run):
    return rows.rearrange("p t (c i) -> p c t i", i=run)


def tile_picked_fkcdjointbdotquad_none_p_kernel(
    tc, x_words, x_scales, w1, gn, w2, gs, offs, n1, n2, n3, n4, n5, cand, n6, n7, out
):
    nc = tc.nc
    with ExitStack() as ctx:
        keep = ctx.enter_context(tc.tile_pool(name="keep", bufs=1))
        psum = ctx.enter_context(tc.psum_pool(name="psum", bufs=1))

        def bank(name, number):
            return psum.tile([P, BANK], F32, name=name, tag=f"bank{number}")

        def load_list(name, source):
            offsets = keep.tile([P, S // LIST_GROUP], U16, name=name)
            nc.sync.dma_start(offsets[:], source)
            return offsets

        def load_gain(name, source):
            gain = keep.tile([P, PACK], F32, name=name)
            nc.sync.dma_start(gain[:], source.rearrange("(p t) o -> p (t o)", t=PACK))
            return gain

        def load_weight_half(name, source, cols):
            half = keep.tile([P, PACK, S // 2], F32, name=name)
            nc.sync.dma_start(half[:], source.rearrange("(p j) c -> p j c", j=PACK)[:, :, cols])
            return half

        offs_sb = load_list("offs_sb", offs)
        cand_sb = load_list("cand_sb", cand)
        table_scales = keep.tile([P, T], U8, name="table_scales")
        nc.gpsimd.memset(table_scales[:].bitcast(I32), 0)
        for q in range(P // QUADRANT):
            nc.sync.dma_start(
                table_scales[QUADRANT * q : QUADRANT * q + 4, :].bitcast(I32),
                x_scales[0, 4 * q : 4 * q + 4, :].bitcast(I32),
            )
        table_words = keep.tile([P, T], I32, name="table_words")
        nc.sync.dma_start(table_words[:], x_words[0].rearrange("p n t -> p (n t)").bitcast(I32))
        w1_raw = [load_weight_half(f"w1_raw{h}", w1, HALVES[h]) for h in range(2)]
        gn_sb = keep.tile([P, PACK], F32, name="gn_sb")
        gn_raw = load_gain("gn_sb_raw", gn)
        nc.gpsimd.tensor_scalar(gn_sb[:], gn_raw[:], 0.75, 0.0, MULT, ADD)
        gs_sb = load_gain("gs_sb", gs)
        w2_raw = [load_weight_half(f"w2_raw{h}", w2, HALVES[h]) for h in range(2)]
        n5_sb = load_list("n5_sb", n5)
        n4_sb = load_list("n4_sb", n4)
        n1_sb = load_list("n1_sb", n1)
        n2_sb = load_list("n2_sb", n2)
        n3_sb = load_list("n3_sb", n3)
        n6_sb = load_list("n6_sb", n6)
        n7_sb = load_list("n7_sb", n7)
        identity = keep.tile([P, P], F32, name="identity")
        make_identity(nc, identity[:])

        def pick(name, table, dtype, offsets):
            picked = keep.tile([P, S], dtype, name=name, align_bytes=64)
            nc.vector.tensor_copy(picked[:], table.indirect(offsets[:]))
            return picked

        def turn(dst, src, start=True, stop=True):
            nc.tensor.matmul(dst, src, identity[:], start=start, stop=stop, is_transpose=True)

        token_scales = pick("token_scales", table_scales[:], U8, offs_sb)

        w1_grouped = keep.tile([P, PACK, P, PACK], BF16, name="w1_grouped", align_bytes=64)
        w1_codes = keep.tile([P, H], U32, name="w1_codes", align_bytes=64)
        w1_scales = keep.tile([P, H], U8, name="w1_scales", align_bytes=64)
        rows_a_half = P // 2
        for copy, h, first, last in (
            (nc.scalar.copy, 0, 0, rows_a_half),
            (nc.scalar.copy, 1, 0, W1_SCALAR_ROWS),
            (nc.vector.tensor_copy, 1, W1_SCALAR_ROWS, rows_a_half),
        ):
            copy(
                w1_grouped[:, :, rows_a_half * h + first : rows_a_half * h + last, :].rearrange("p t m j -> p m j t"),
                w1_raw[h][:, :, PACK * first : PACK * last].rearrange("p j (m t) -> p m j t", t=PACK),
            )
        for t in (0, 2):
            cols = slice(t * P, (t + 2) * P)
            nc.vector.quantize_mx(
                w1_codes[:, cols].bitcast(FP8X4),
                w1_scales[:, cols],
                w1_grouped[:, t : t + 2].rearrange("p t m j -> p (t m j)"),
            )
        token_words = pick("token_words", table_words[:].bitcast(U32), U32, offs_sb)
        cand_scales = pick("cand_scales", table_scales[:], U8, cand_sb)
        cand_words = pick("cand_words", table_words[:].bitcast(U32), U32, cand_sb)

        w2_grouped = keep.tile([P, N, PACK], BF16, name="w2_grouped", tag="w1_grouped", align_bytes=64)
        w2_codes = keep.tile([P, N], U32, name="w2_codes", align_bytes=64)
        w2_scales = keep.tile([P, N], U8, name="w2_scales", align_bytes=64)
        for cols, raw in zip(HALVES, w2_raw):
            nc.vector.tensor_copy(interleaved(w2_grouped[:, cols], LINE), by_rows(raw[:], LINE))

        gs_bank = bank("gs_row_bank", 4)
        for t in range(PACK):
            turn(gs_bank[:, t * P : (t + 1) * P], gs_sb[:, t : t + 1].to_broadcast([P, P]))
        gs_row = keep.tile([P, 2, P, 2], F32, name="gs_row", tag="w1_raw1")
        nc.scalar.activation(gs_row[:], gs_bank[:].rearrange("j (u e p) -> j u p e", u=2, e=2), COPY, scale=0.75)

        p1 = keep.tile([P, PACK, S], F32, name="p1")
        y, y_gn = [], []
        for t in range(PACK):
            y_bank = bank(f"y_bank{t}", t)
            product(nc, y_bank, (w1_codes, w1_scales), t, (token_words, token_scales))
            y_t = keep.tile([P, WINDOW], F32, name=f"y{t}")
            y_gn_t = keep.tile([P, WINDOW], F32, name=f"y_gn{t}")
            nc.scalar.activation(y_t[:, :S], y_bank[:], COPY)
            nc.vector.tensor_scalar(y_gn_t[:, :S], y_t[:, :S], gn_sb[:, t : t + 1], None, MULT)
            y.append(y_t)
            y_gn.append(y_gn_t)

        def turn_tile(banks, e, source, start=False, stop=False):
            for h in range(2):
                for g in range(2):
                    cols = slice((2 * h + g) * P, (2 * h + g + 1) * P)
                    dst = banks[h][:, (2 * g + e) * P : (2 * g + e + 1) * P]
                    turn(dst, source[:, cols], start=start and g == 0, stop=stop and g == 1)

        def pairs(turned):
            return turned[:].rearrange("j (g e p) -> j g p e", g=2, e=2)

        z2_rounded = []
        for u in range(2):
            first_bank = (4, 0)[u]
            d4 = [bank(f"d4_{u}{h}", first_bank + h) for h in range(2)]
            d5 = [bank(f"d5_{u}{h}", first_bank + 2 + h) for h in range(2)]
            for e in range(2):
                turn_tile(d5, e, y[2 * u + e], start=e == 0)
                turn_tile(d4, e, y[2 * u + e], start=e == 0)
            for e in range(2):
                t = 2 * u + e
                minus_n4 = keep.tile([P, S], F32, name=f"minus_n4_{t}")
                minus_n5 = keep.tile([P, S], F32, name=f"minus_n5_{t}")
                if t == N5_TILE_ON_VECTOR:
                    nc.vector.tensor_scalar(minus_n5[:], y[t][:].indirect(n5_sb[:]), -1.0, 0.0, MULT, ADD)
                else:
                    nc.scalar.activation(minus_n5[:], y[t][:].indirect(n5_sb[:]), COPY, scale=-1.0)
                nc.scalar.activation(minus_n4[:], y[t][:].indirect(n4_sb[:]), COPY, scale=-1.0)
                turn_tile(d5, e, minus_n5, stop=e == 1)
                turn_tile(d4, e, minus_n4, stop=e == 1)
            if u == 0:
                for t in range(PACK):
                    nc.vector.tensor_tensor(p1[:, t], y[t][:].indirect(n1_sb[:]), y_gn[t][:, :S], MULT)
                nc.vector.quantize_mx(
                    w2_codes[:].bitcast(FP8X4), w2_scales[:], w2_grouped[:].rearrange("p c j -> p (c j)")
                )
            gs_pairs = gs_row[:, u].unsqueeze(1).to_broadcast([P, 2, P, 2])
            scaled = [keep.tile([P, 2, P, 2], F32, name=f"scaled{u}{h}", align_bytes=64) for h in range(2)]
            for h in range(2):
                nc.vector.tensor_tensor(scaled[h][:], pairs(d5[h]), gs_pairs, MULT)
            rounded = [keep.tile([P, 2, P, 2], BF16, name=f"z2_rounded{u}{h}") for h in range(2)]
            for h in range(2):
                nc.vector.tensor_tensor(rounded[h][:], pairs(d4[h]), scaled[h][:], MULT)
            z2_rounded.append(rounded)

        z2_back = [bank(f"z2_back{h}", 6 + h) for h in range(2)]
        for u in range(2):
            for h in range(2):
                as_f32 = z2_rounded[u][h][:].rearrange("j g p e -> j (g p e)").bitcast(F32)
                for g in range(2):
                    turn(z2_back[h][:, (2 * u + g) * P : (2 * u + g + 1) * P], as_f32[:, g * P : (g + 1) * P])
        z2_codes = keep.tile([P, S], U32, name="z2_codes", align_bytes=64)
        z2_scales = keep.tile([P, S], U8, name="z2_scales", align_bytes=64)
        for h, cols in enumerate(HALVES):
            grouped = keep.tile([P, S // 2, PACK], BF16, name=f"z2_grouped{h}", align_bytes=64)
            nc.scalar.copy(grouped[:].bitcast(F32), z2_back[h][:].rearrange("p (u j) -> p j u", u=2))
            nc.vector.quantize_mx(
                z2_codes[:, cols].bitcast(FP8X4), z2_scales[:, cols], grouped[:].rearrange("p j t -> p (j t)")
            )

        b_banks = []
        for m, number in enumerate((4, 5, 2, 3)):
            b_bank = bank(f"b_bank{m}", number)
            product(nc, b_bank, (cand_words, cand_scales), m, (z2_codes, z2_scales))
            b_banks.append(b_bank)

        p3 = keep.tile([P, PACK, S], F32, name="p3", tag="scaled10", align_bytes=64)
        for t, tag in enumerate(("at_n2_0", "at_n2_1", "z2_rounded10", "z2_rounded11")):
            at_n2 = keep.tile([P, S], F32, name=f"at_n2_{t}", tag=tag)
            nc.scalar.activation(at_n2[:], y_gn[t][:].indirect(n2_sb[:]), COPY)
            nc.vector.tensor_tensor(p3[:, t], y[t][:].indirect(n3_sb[:]), at_n2[:], MULT)
        z_codes = keep.tile([P, S], U32, name="z_codes", align_bytes=64)
        z_scales = keep.tile([P, S], U8, name="z_scales", align_bytes=64)
        z_grouped = [keep.tile([P, S // 2, PACK], BF16, name=f"z_grouped{h}", align_bytes=64) for h in range(2)]
        for grouped, cols in zip(z_grouped, HALVES):
            nc.vector.tensor_tensor(
                interleaved(grouped[:], 2), by_rows(p1[:, :, cols], 2), by_rows(p3[:, :, cols], 2), ADD
            )
        for grouped, cols in zip(z_grouped, HALVES):
            nc.vector.quantize_mx(
                z_codes[:, cols].bitcast(FP8X4), z_scales[:, cols], grouped[:].rearrange("p j t -> p (j t)")
            )

        gaps = []
        for m in range(C // P):
            b_m = keep.tile([P, WINDOW], F32, name=f"b{m}")
            at_n6 = keep.tile([P, S], F32, name=f"at_n6_{m}")
            gap = keep.tile([P, S], F32, name=f"gap{m}")
            nc.scalar.activation(b_m[:, :S], b_banks[m][:], COPY)
            nc.scalar.activation(at_n6[:], b_m[:].indirect(n6_sb[:]), COPY)
            if m == N7_TILE_ON_SCALAR:
                at_n7 = keep.tile([P, S], F32, name=f"at_n7_{m}")
                nc.scalar.activation(at_n7[:], b_m[:].indirect(n7_sb[:]), COPY)
                nc.vector.tensor_tensor(gap[:], at_n7[:], at_n6[:], SUBTRACT)
            else:
                nc.vector.tensor_tensor(gap[:], b_m[:].indirect(n7_sb[:]), at_n6[:], SUBTRACT)
            gaps.append(gap)

        for m, number in enumerate((0, 1, 6, 7)):
            a_bank = bank(f"a_bank{m}", number)
            product(nc, a_bank, (w2_codes, w2_scales), m, (z_codes, z_scales))
            gate = keep.tile([P, S], F32, name=f"gate{m}")
            result = keep.tile([P, S], F32, name=f"result{m}")
            for cols in HALVES if m == N // P - 1 else (slice(0, S),):
                nc.scalar.activation(gate[:, cols], gaps[m][:, cols], TANH, scale=-0.0625)
                nc.vector.tensor_tensor(result[:, cols], a_bank[:, cols], gate[:, cols], MULT)
                nc.sync.dma_start(out[m * P : (m + 1) * P, cols], result[:, cols])
